import numpy as np, ml_dtypes
CORES = [2,3,6,7,58,59,62,63,114,115,118,119]
N = 12
F = 128
BETA, LR = 0.75, 0.5
def setup_inputs(rng):
    return {"gr": rng.standard_normal((N, 128, N * F), dtype=np.float32).astype(ml_dtypes.bfloat16), "m": rng.standard_normal((N, 128, F), dtype=np.float32).astype(ml_dtypes.bfloat16), "w": rng.standard_normal((N, 128, F), dtype=np.float32).astype(ml_dtypes.bfloat16)}
def reference(gr, m, w):
    GR, M, W = gr.astype(np.float64), m.astype(np.float64), w.astype(np.float64)
    s = GR.sum(axis=0)
    m2 = np.stack([BETA * M[r] + s[:, F * r:F * r + F] for r in range(N)])
    w2 = np.concatenate([W[r] - LR * m2[r] for r in range(N)], axis=1)
    return {"y": np.broadcast_to(w2.astype(ml_dtypes.bfloat16), (N, 128, N * F)), "mo": m2.astype(ml_dtypes.bfloat16)}

@@ -1,0 +1,192 @@
+from concourse.bass import DstId, RemoteDMATransfer
+from concourse.mybir import AluOpType
+
+F = 128
+NB = 12
+PP = 4
+BP = NB // PP
+PW = BP * F
+
+SCRATCH = {
+    "G": ("sbuf", [128, NB * F], "bfloat16"),
+    "M": ("sbuf", [128, F], "bfloat16"),
+    "W": ("sbuf", [128, F], "bfloat16"),
+    "C75": ("sbuf", [128, F], "bfloat16"),
+    "CN2": ("sbuf", [128, F], "bfloat16"),
+    "CH": ("sbuf", [128, PW], "bfloat16"),
+    "PA": ("sbuf", [128, PW], "bfloat16"),
+    "PB": ("sbuf", [128, PW], "bfloat16"),
+    "L": ("sbuf", [128, PP * PW], "bfloat16"),
+    "R": ("sbuf", [128, 3 * PW], "bfloat16"),
+    "ACC": ("psum", [128, PW], "float32"),
+    "Y": ("sbuf", [128, NB * F], "bfloat16"),
+    "U": ("sbuf", [128, F], "float32"),
+    "MO": ("sbuf", [128, F], "bfloat16"),
+}
+SEMAPHORES = ["ldg", "ldm", "ldw", "vk", "pb", "s1", "va", "rs0", "rs1", "rs2", "wr",
+              "ya0", "ya1", "ya2", "ya3", "mr", "sty", "stm", "sent"]
+
+
+def _bits(mask):
+    return [b for b in range(mask.bit_length()) if (mask >> b) & 1]
+
+
+def _mk(bs):
+    m = 0
+    for b in bs:
+        m |= 1 << b
+    return m
+
+
+def rank_program(g, core, T, topo):
+    rank = T.rank_of(core)
+    if rank is None:
+        return
+    v, sy, sc = g.vector, g.sync, g.scalar
+    S = T.sem
+
+    chips = sorted(set(topo.chip(c) for c in T.cores))
+    members = [sorted([c for c in T.cores if topo.chip(c) == ch], key=lambda c: (topo.die(c), c)) for ch in chips]
+    X = chips.index(topo.chip(core))
+    mine = members[X]
+    p = mine.index(core)
+
+    def dst_id(c):
+        rid, pid, _ = topo.addr(c)
+        return DstId(rid=rid, pnc=pid)
+
+    def piece(t, q):
+        return t[:, q * PW:(q + 1) * PW]
+
+    def common(src, dsts):
+        m = topo.mask(src, dsts[0])
+        for d in dsts:
+            m &= topo.mask(src, d)
+        return m
+
+    def s1_plan(c):
+        pc = mine.index(c)
+        hc = T.rank_of(c) // BP
+        oth = [q for q in range(PP) if q != pc]
+        if hc != pc:
+            last, fold = hc, True
+        else:
+            far = [q for q in oth if topo.die(mine[q]) != topo.die(c)]
+            last, fold = (far or oth)[-1], False
+        return [q for q in oth if q != last], last, fold
+
+    def s1_masks(c):
+        first, last, _ = s1_plan(c)
+        both = _bits(common(c, [mine[q] for q in first]))
+        return {first[0]: _mk(both[0::2]), first[1]: _mk(both[1::2]), last: topo.mask(c, mine[last])}
+
+    hq, slot = rank // BP, rank % BP
+    own = hq == p
+    sl = slice(slot * F, (slot + 1) * F)
+    peers = [q for q in range(PP) if q != p]
+    others = [x for x in range(len(chips)) if x != X]
+    sent = 0
+
+    sy.dma_start(T.G[:], T.gr[:]).then_inc(S.ldg, 16)
+    sc.dma_start(T.M[:], T.m[:]).then_inc(S.ldm, 16)
+    sc.dma_start(T.W[:], T.w[:]).then_inc(S.ldw, 16)
+
+    v.memset(T.C75[:], 0.75).then_inc(S.vk, 1)
+    v.memset(T.CN2[:], -2.0).then_inc(S.vk, 1)
+    npb = 0
+    for t in (T.PA, T.PB):
+        for s in range(BP):
+            if s != slot:
+                v.memset(t[:, s * F:(s + 1) * F], 0.0).then_inc(S.pb, 1)
+                npb += 1
+    v.memset(T.CH[:], -0.5).then_inc(S.vk, 1)
+    v.wait_ge(S.vk, 3)
+    v.wait_ge(S.ldm, 16)
+    v.tensor_tensor(T.PA[:, sl], T.M[:], T.C75[:], AluOpType.mult).then_inc(S.pb, 1)
+    v.wait_ge(S.ldw, 16)
+    v.tensor_tensor(T.PB[:, sl], T.W[:], T.CN2[:], AluOpType.mult).then_inc(S.pb, 1)
+    npb += 2
+
+    first, last, fold = s1_plan(core)
+    mk = s1_masks(core)
+    g.wait_ge(S.ldg, 16)
+    g.remote_dma_fused(
+        [RemoteDMATransfer(dst_ids=[dst_id(mine[q])], dma_engine_mask=mk[q], remote_sem=S.s1,
+                           src=piece(T.G, q), dst=piece(T.L, p)) for q in first],
+        local_sem=S.sent)
+    sent += sum(len(_bits(mk[q])) for q in first)
+    if fold:
+        g.wait_ge(S.pb, npb)
+        tr = RemoteDMATransfer(dst_ids=[dst_id(mine[last])], dma_engine_mask=mk[last], remote_sem=S.s1,
+                               srcs=[piece(T.G, last), T.PA[:], T.PB[:]], dsts=[piece(T.L, p)], alu_op=1)
+    else:
+        tr = RemoteDMATransfer(dst_ids=[dst_id(mine[last])], dma_engine_mask=mk[last], remote_sem=S.s1,
+                               src=piece(T.G, last), dst=piece(T.L, p))
+    g.remote_dma_fused([tr], local_sem=S.sent)
+    sent += len(_bits(mk[last]))
+    s1tot = sum(len(_bits(s1_masks(mine[q])[p])) for q in peers)
+
+    def m2(x):
+        return common(members[x][p], [members[z][p] for z in range(len(chips)) if z != x])
+
+    srcs = [piece(T.G, p)] + [piece(T.L, q) for q in peers]
+    if own:
+        g.wait_ge(S.pb, npb)
+        srcs += [T.PA[:], T.PB[:]]
+    g.wait_ge(S.s1, s1tot)
+    g.remote_dma_fused(
+        [RemoteDMATransfer(dst_ids=[dst_id(members[x][p]) for x in others], dma_engine_mask=m2(X),
+                           remote_sem=S["rs%d" % X], srcs=srcs, dsts=[piece(T.R, X) for x in others], alu_op=1)],
+        local_sem=S.sent)
+    sent += len(_bits(m2(X)))
+
+    nva = [0]
+
+    def acc(out, a, b, op=AluOpType.add):
+        if nva[0]:
+            v.wait_ge(S.va, nva[0])
+        v.tensor_tensor(out, a, b, op).then_inc(S.va, 1)
+        nva[0] += 1
+
+    v.wait_ge(S.ldg, 16)
+    v.wait_ge(S.s1, s1tot)
+    acc(T.ACC[:], piece(T.G, p), piece(T.L, peers[0]))
+    acc(T.ACC[:], T.ACC[:], piece(T.L, peers[1]))
+    acc(T.ACC[:], T.ACC[:], piece(T.L, peers[2]))
+    if own:
+        v.wait_ge(S.pb, npb)
+        acc(T.ACC[:, sl], T.ACC[:, sl], T.PA[:, sl])
+        acc(T.ACC[:, sl], T.ACC[:, sl], T.PB[:, sl])
+    for x in sorted(others, key=lambda x: (not topo.same_plane(chips[x], chips[X]), x)):
+        v.wait_ge(S["rs%d" % x], len(_bits(m2(x))))
+        acc(T.ACC[:], T.ACC[:], piece(T.R, x))
+    v.wait_ge(S.va, nva[0])
+    v.tensor_tensor(piece(T.Y, p), T.ACC[:], T.CH[:], AluOpType.mult).then_inc(S.wr, 1)
+    if own:
+        v.tensor_tensor(T.MO[:], T.ACC[:, sl], T.PB[:, sl], AluOpType.subtract).then_inc(S.mr, 1)
+
+    def m3(q):
+        return common(mine[q], [mine[t] for t in range(PP) if t != q])
+
+    g.wait_ge(S.wr, 1)
+    g.remote_dma_fused(
+        [RemoteDMATransfer(dst_ids=[dst_id(mine[q]) for q in peers], dma_engine_mask=m3(p),
+                           remote_sem=S["ya%d" % p], srcs=[piece(T.Y, p)], dsts=[piece(T.Y, p) for q in peers])],
+        local_sem=S.sent)
+    sent += len(_bits(m3(p)))
+
+    if not own:
+        v.wait_ge(S["ya%d" % hq], len(_bits(m3(hq))))
+        acc(T.U[:], T.W[:], T.Y[:, rank * F:(rank + 1) * F], AluOpType.subtract)
+        v.wait_ge(S.va, nva[0])
+        v.tensor_tensor(T.MO[:], T.U[:], T.U[:], AluOpType.add).then_inc(S.mr, 1)
+
+    sy.wait_ge(S.wr, 1)
+    for q in peers:
+        sy.wait_ge(S["ya%d" % q], len(_bits(m3(q))))
+    sy.dma_start(T.y[:], T.Y[:]).then_inc(S.sty, 16)
+    sc.wait_ge(S.mr, 1)
+    sc.dma_start(T.mo[:], T.MO[:]).then_inc(S.stm, 16)
+    sy.wait_ge(S.sty, 16)
+    sc.wait_ge(S.stm, 16)
+    g.wait_ge(S.sent, sent)

@@ -23,8 +23,10 @@ SCRATCH = {
     "U": ("sbuf", [128, F], "float32"),
     "MO": ("sbuf", [128, F], "bfloat16"),
 }
-SEMAPHORES = ["ldg", "ldm", "ldw", "vk", "pb", "s1", "va", "rs0", "rs1", "rs2", "wr",
+SEMAPHORES = ["ld1", "ldc", "ldo", "ldm", "ldw", "vk", "pb", "s1", "va", "rs0", "rs1", "rs2", "wr",
               "ya0", "ya1", "ya2", "ya3", "mr", "sty", "stm", "sent"]
+
+_P3 = ((0, 1, 2), (0, 2, 1), (1, 0, 2), (1, 2, 0), (2, 0, 1), (2, 1, 0))
 
 
 def _bits(mask):
@@ -38,6 +40,25 @@ def _mk(bs):
     return m
 
 
+def _gather_order(want):
+    peers = [[t for t in range(PP) if t != q] for q in range(PP)]
+    best, bestc = None, None
+    for a in _P3:
+        for b in _P3:
+            for c in _P3:
+                for d in _P3:
+                    o = [[peers[q][i] for i in pm] for q, pm in enumerate((a, b, c, d))]
+                    cost = 0
+                    for t in range(PP):
+                        places = [o[q].index(t) for q in range(PP) if q != t]
+                        cost += 100 * (3 - len(set(places)))
+                        if want[t] is not None:
+                            cost += o[want[t]].index(t) ** 2
+                    if bestc is None or cost < bestc:
+                        best, bestc = o, cost
+    return best
+
+
 def rank_program(g, core, T, topo):
     rank = T.rank_of(core)
     if rank is None:
@@ -46,6 +67,7 @@ def rank_program(g, core, T, topo):
     S = T.sem
 
     chips = sorted(set(topo.chip(c) for c in T.cores))
+    NC = len(chips)
     members = [sorted([c for c in T.cores if topo.chip(c) == ch], key=lambda c: (topo.die(c), c)) for ch in chips]
     X = chips.index(topo.chip(core))
     mine = members[X]
@@ -84,12 +106,16 @@ def rank_program(g, core, T, topo):
     own = hq == p
     sl = slice(slot * F, (slot + 1) * F)
     peers = [q for q in range(PP) if q != p]
-    others = [x for x in range(len(chips)) if x != X]
+    first, last, fold = s1_plan(core)
+    mk = s1_masks(core)
     sent = 0
 
-    sy.dma_start(T.G[:], T.gr[:]).then_inc(S.ldg, 16)
-    sc.dma_start(T.M[:], T.m[:]).then_inc(S.ldm, 16)
+    sy.dma_start(piece(T.G, first[0]), piece(T.gr, first[0])).then_inc(S.ld1, 16)
+    sc.dma_start(piece(T.G, first[1]), piece(T.gr, first[1])).then_inc(S.ld1, 16)
+    sy.dma_start(T.M[:], T.m[:]).then_inc(S.ldm, 16)
     sc.dma_start(T.W[:], T.w[:]).then_inc(S.ldw, 16)
+    sy.dma_start(piece(T.G, last), piece(T.gr, last)).then_inc(S.ldc, 16)
+    sc.dma_start(piece(T.G, p), piece(T.gr, p)).then_inc(S.ldo, 16)
 
     v.memset(T.C75[:], 0.75).then_inc(S.vk, 1)
     v.memset(T.CN2[:], -2.0).then_inc(S.vk, 1)
@@ -107,14 +133,13 @@ def rank_program(g, core, T, topo):
     v.tensor_tensor(T.PB[:, sl], T.W[:], T.CN2[:], AluOpType.mult).then_inc(S.pb, 1)
     npb += 2
 
-    first, last, fold = s1_plan(core)
-    mk = s1_masks(core)
-    g.wait_ge(S.ldg, 16)
+    g.wait_ge(S.ld1, 32)
     g.remote_dma_fused(
         [RemoteDMATransfer(dst_ids=[dst_id(mine[q])], dma_engine_mask=mk[q], remote_sem=S.s1,
                            src=piece(T.G, q), dst=piece(T.L, p)) for q in first],
         local_sem=S.sent)
     sent += sum(len(_bits(mk[q])) for q in first)
+    g.wait_ge(S.ldc, 16)
     if fold:
         g.wait_ge(S.pb, npb)
         tr = RemoteDMATransfer(dst_ids=[dst_id(mine[last])], dma_engine_mask=mk[last], remote_sem=S.s1,
@@ -127,16 +152,19 @@ def rank_program(g, core, T, topo):
     s1tot = sum(len(_bits(s1_masks(mine[q])[p])) for q in peers)
 
     def m2(x):
-        return common(members[x][p], [members[z][p] for z in range(len(chips)) if z != x])
+        return common(members[x][p], [members[z][p] for z in range(NC) if z != x])
 
+    to = [(X + k) % NC for k in range(1, NC)]
+    frm = [(X - k) % NC for k in range(1, NC)]
     srcs = [piece(T.G, p)] + [piece(T.L, q) for q in peers]
+    g.wait_ge(S.ldo, 16)
     if own:
         g.wait_ge(S.pb, npb)
         srcs += [T.PA[:], T.PB[:]]
     g.wait_ge(S.s1, s1tot)
     g.remote_dma_fused(
-        [RemoteDMATransfer(dst_ids=[dst_id(members[x][p]) for x in others], dma_engine_mask=m2(X),
-                           remote_sem=S["rs%d" % X], srcs=srcs, dsts=[piece(T.R, X) for x in others], alu_op=1)],
+        [RemoteDMATransfer(dst_ids=[dst_id(members[x][p]) for x in to], dma_engine_mask=m2(X),
+                           remote_sem=S["rs%d" % X], srcs=srcs, dsts=[piece(T.R, X) for x in to], alu_op=1)],
         local_sem=S.sent)
     sent += len(_bits(m2(X)))
 
@@ -148,7 +176,7 @@ def rank_program(g, core, T, topo):
         v.tensor_tensor(out, a, b, op).then_inc(S.va, 1)
         nva[0] += 1
 
-    v.wait_ge(S.ldg, 16)
+    v.wait_ge(S.ldo, 16)
     v.wait_ge(S.s1, s1tot)
     acc(T.ACC[:], piece(T.G, p), piece(T.L, peers[0]))
     acc(T.ACC[:], T.ACC[:], piece(T.L, peers[1]))
@@ -157,7 +185,7 @@ def rank_program(g, core, T, topo):
         v.wait_ge(S.pb, npb)
         acc(T.ACC[:, sl], T.ACC[:, sl], T.PA[:, sl])
         acc(T.ACC[:, sl], T.ACC[:, sl], T.PB[:, sl])
-    for x in sorted(others, key=lambda x: (not topo.same_plane(chips[x], chips[X]), x)):
+    for x in frm:
         v.wait_ge(S["rs%d" % x], len(_bits(m2(x))))
         acc(T.ACC[:], T.ACC[:], piece(T.R, x))
     v.wait_ge(S.va, nva[0])
@@ -168,10 +196,12 @@ def rank_program(g, core, T, topo):
     def m3(q):
         return common(mine[q], [mine[t] for t in range(PP) if t != q])
 
+    want = [T.rank_of(c) // BP for c in mine]
+    order = _gather_order([None if want[t] == t else want[t] for t in range(PP)])
     g.wait_ge(S.wr, 1)
     g.remote_dma_fused(
-        [RemoteDMATransfer(dst_ids=[dst_id(mine[q]) for q in peers], dma_engine_mask=m3(p),
-                           remote_sem=S["ya%d" % p], srcs=[piece(T.Y, p)], dsts=[piece(T.Y, p) for q in peers])],
+        [RemoteDMATransfer(dst_ids=[dst_id(mine[q]) for q in order[p]], dma_engine_mask=m3(p),
+                           remote_sem=S["ya%d" % p], srcs=[piece(T.Y, p)], dsts=[piece(T.Y, p) for q in order[p]])],
         local_sem=S.sent)
     sent += len(_bits(m3(p)))
 
@@ -181,12 +211,30 @@ def rank_program(g, core, T, topo):
         v.wait_ge(S.va, nva[0])
         v.tensor_tensor(T.MO[:], T.U[:], T.U[:], AluOpType.add).then_inc(S.mr, 1)
 
+    arr = sorted(peers, key=lambda q: order[q].index(p))
+    nsy = nsc = 0
+
+    def put_mo():
+        sy.wait_ge(S.mr, 1)
+        sy.dma_start(T.mo[:], T.MO[:]).then_inc(S.sty, 16)
+
     sy.wait_ge(S.wr, 1)
-    for q in peers:
-        sy.wait_ge(S["ya%d" % q], len(_bits(m3(q))))
-    sy.dma_start(T.y[:], T.Y[:]).then_inc(S.sty, 16)
-    sc.wait_ge(S.mr, 1)
-    sc.dma_start(T.mo[:], T.MO[:]).then_inc(S.stm, 16)
-    sy.wait_ge(S.sty, 16)
-    sc.wait_ge(S.stm, 16)
+    sy.dma_start(piece(T.y, p), piece(T.Y, p)).then_inc(S.sty, 16)
+    nsy += 16
+    if own:
+        put_mo()
+        nsy += 16
+    for k, q in enumerate(arr):
+        eng, sem = ((sc, S.stm), (sy, S.sty), (sc, S.stm))[k]
+        eng.wait_ge(S["ya%d" % q], len(_bits(m3(q))))
+        eng.dma_start(piece(T.y, q), piece(T.Y, q)).then_inc(sem, 16)
+        if k == 1:
+            nsy += 16
+        else:
+            nsc += 16
+    if not own:
+        put_mo()
+        nsy += 16
+    sy.wait_ge(S.sty, nsy)
+    sc.wait_ge(S.stm, nsc)
     g.wait_ge(S.sent, sent)

from concourse.bass import DstId, RemoteDMATransfer
from concourse.mybir import AluOpType

F = 128
NB = 12
PP = 4
BP = NB // PP
PW = BP * F

SCRATCH = {
    "G": ("sbuf", [128, NB * F], "bfloat16"),
    "M": ("sbuf", [128, F], "bfloat16"),
    "W": ("sbuf", [128, F], "bfloat16"),
    "C75": ("sbuf", [128, F], "bfloat16"),
    "CN2": ("sbuf", [128, F], "bfloat16"),
    "CH": ("sbuf", [128, PW], "bfloat16"),
    "PA": ("sbuf", [128, PW], "bfloat16"),
    "PB": ("sbuf", [128, PW], "bfloat16"),
    "L": ("sbuf", [128, PP * PW], "bfloat16"),
    "R": ("sbuf", [128, 3 * PW], "bfloat16"),
    "ACC": ("psum", [128, PW], "float32"),
    "Y": ("sbuf", [128, NB * F], "bfloat16"),
    "U": ("sbuf", [128, F], "float32"),
    "MO": ("sbuf", [128, F], "bfloat16"),
}
SEMAPHORES = ["ld1", "ldc", "ldo", "ldm", "ldw", "vk", "pb", "s1", "va", "rs0", "rs1", "rs2", "wr",
              "ya0", "ya1", "ya2", "ya3", "mr", "sty", "stm", "sent"]

_P3 = ((0, 1, 2), (0, 2, 1), (1, 0, 2), (1, 2, 0), (2, 0, 1), (2, 1, 0))


def _bits(mask):
    return [b for b in range(mask.bit_length()) if (mask >> b) & 1]


def _mk(bs):
    m = 0
    for b in bs:
        m |= 1 << b
    return m


def _gather_order(want):
    peers = [[t for t in range(PP) if t != q] for q in range(PP)]
    best, bestc = None, None
    for a in _P3:
        for b in _P3:
            for c in _P3:
                for d in _P3:
                    o = [[peers[q][i] for i in pm] for q, pm in enumerate((a, b, c, d))]
                    cost = 0
                    for t in range(PP):
                        places = [o[q].index(t) for q in range(PP) if q != t]
                        cost += 100 * (3 - len(set(places)))
                        if want[t] is not None:
                            cost += o[want[t]].index(t) ** 2
                    if bestc is None or cost < bestc:
                        best, bestc = o, cost
    return best


def rank_program(g, core, T, topo):
    rank = T.rank_of(core)
    if rank is None:
        return
    v, sy, sc = g.vector, g.sync, g.scalar
    S = T.sem

    chips = sorted(set(topo.chip(c) for c in T.cores))
    NC = len(chips)
    members = [sorted([c for c in T.cores if topo.chip(c) == ch], key=lambda c: (topo.die(c), c)) for ch in chips]
    X = chips.index(topo.chip(core))
    mine = members[X]
    p = mine.index(core)

    def dst_id(c):
        rid, pid, _ = topo.addr(c)
        return DstId(rid=rid, pnc=pid)

    def piece(t, q):
        return t[:, q * PW:(q + 1) * PW]

    def common(src, dsts):
        m = topo.mask(src, dsts[0])
        for d in dsts:
            m &= topo.mask(src, d)
        return m

    def s1_plan(c):
        pc = mine.index(c)
        hc = T.rank_of(c) // BP
        oth = [q for q in range(PP) if q != pc]
        if hc != pc:
            last, fold = hc, True
        else:
            far = [q for q in oth if topo.die(mine[q]) != topo.die(c)]
            last, fold = (far or oth)[-1], False
        return [q for q in oth if q != last], last, fold

    def s1_masks(c):
        first, last, _ = s1_plan(c)
        both = _bits(common(c, [mine[q] for q in first]))
        return {first[0]: _mk(both[0::2]), first[1]: _mk(both[1::2]), last: topo.mask(c, mine[last])}

    hq, slot = rank // BP, rank % BP
    own = hq == p
    sl = slice(slot * F, (slot + 1) * F)
    peers = [q for q in range(PP) if q != p]
    first, last, fold = s1_plan(core)
    mk = s1_masks(core)
    sent = 0

    sy.dma_start(piece(T.G, first[0]), piece(T.gr, first[0])).then_inc(S.ld1, 16)
    sc.dma_start(piece(T.G, first[1]), piece(T.gr, first[1])).then_inc(S.ld1, 16)
    sy.dma_start(T.M[:], T.m[:]).then_inc(S.ldm, 16)
    sc.dma_start(T.W[:], T.w[:]).then_inc(S.ldw, 16)
    sy.dma_start(piece(T.G, last), piece(T.gr, last)).then_inc(S.ldc, 16)
    sc.dma_start(piece(T.G, p), piece(T.gr, p)).then_inc(S.ldo, 16)

    v.memset(T.C75[:], 0.75).then_inc(S.vk, 1)
    v.memset(T.CN2[:], -2.0).then_inc(S.vk, 1)
    npb = 0
    for t in (T.PA, T.PB):
        for s in range(BP):
            if s != slot:
                v.memset(t[:, s * F:(s + 1) * F], 0.0).then_inc(S.pb, 1)
                npb += 1
    v.memset(T.CH[:], -0.5).then_inc(S.vk, 1)
    v.wait_ge(S.vk, 3)
    v.wait_ge(S.ldm, 16)
    v.tensor_tensor(T.PA[:, sl], T.M[:], T.C75[:], AluOpType.mult).then_inc(S.pb, 1)
    v.wait_ge(S.ldw, 16)
    v.tensor_tensor(T.PB[:, sl], T.W[:], T.CN2[:], AluOpType.mult).then_inc(S.pb, 1)
    npb += 2

    g.wait_ge(S.ld1, 32)
    g.remote_dma_fused(
        [RemoteDMATransfer(dst_ids=[dst_id(mine[q])], dma_engine_mask=mk[q], remote_sem=S.s1,
                           src=piece(T.G, q), dst=piece(T.L, p)) for q in first],
        local_sem=S.sent)
    sent += sum(len(_bits(mk[q])) for q in first)
    g.wait_ge(S.ldc, 16)
    if fold:
        g.wait_ge(S.pb, npb)
        tr = RemoteDMATransfer(dst_ids=[dst_id(mine[last])], dma_engine_mask=mk[last], remote_sem=S.s1,
                               srcs=[piece(T.G, last), T.PA[:], T.PB[:]], dsts=[piece(T.L, p)], alu_op=1)
    else:
        tr = RemoteDMATransfer(dst_ids=[dst_id(mine[last])], dma_engine_mask=mk[last], remote_sem=S.s1,
                               src=piece(T.G, last), dst=piece(T.L, p))
    g.remote_dma_fused([tr], local_sem=S.sent)
    sent += len(_bits(mk[last]))
    s1tot = sum(len(_bits(s1_masks(mine[q])[p])) for q in peers)

    def m2(x):
        return common(members[x][p], [members[z][p] for z in range(NC) if z != x])

    to = [(X + k) % NC for k in range(1, NC)]
    frm = [(X - k) % NC for k in range(1, NC)]
    srcs = [piece(T.G, p)] + [piece(T.L, q) for q in peers]
    g.wait_ge(S.ldo, 16)
    if own:
        g.wait_ge(S.pb, npb)
        srcs += [T.PA[:], T.PB[:]]
    g.wait_ge(S.s1, s1tot)
    g.remote_dma_fused(
        [RemoteDMATransfer(dst_ids=[dst_id(members[x][p]) for x in to], dma_engine_mask=m2(X),
                           remote_sem=S["rs%d" % X], srcs=srcs, dsts=[piece(T.R, X) for x in to], alu_op=1)],
        local_sem=S.sent)
    sent += len(_bits(m2(X)))

    nva = [0]

    def acc(out, a, b, op=AluOpType.add):
        if nva[0]:
            v.wait_ge(S.va, nva[0])
        v.tensor_tensor(out, a, b, op).then_inc(S.va, 1)
        nva[0] += 1

    v.wait_ge(S.ldo, 16)
    v.wait_ge(S.s1, s1tot)
    acc(T.ACC[:], piece(T.G, p), piece(T.L, peers[0]))
    acc(T.ACC[:], T.ACC[:], piece(T.L, peers[1]))
    acc(T.ACC[:], T.ACC[:], piece(T.L, peers[2]))
    if own:
        v.wait_ge(S.pb, npb)
        acc(T.ACC[:, sl], T.ACC[:, sl], T.PA[:, sl])
        acc(T.ACC[:, sl], T.ACC[:, sl], T.PB[:, sl])
    for x in frm:
        v.wait_ge(S["rs%d" % x], len(_bits(m2(x))))
        acc(T.ACC[:], T.ACC[:], piece(T.R, x))
    v.wait_ge(S.va, nva[0])
    v.tensor_tensor(piece(T.Y, p), T.ACC[:], T.CH[:], AluOpType.mult).then_inc(S.wr, 1)
    if own:
        v.tensor_tensor(T.MO[:], T.ACC[:, sl], T.PB[:, sl], AluOpType.subtract).then_inc(S.mr, 1)

    def m3(q):
        return common(mine[q], [mine[t] for t in range(PP) if t != q])

    want = [T.rank_of(c) // BP for c in mine]
    order = _gather_order([None if want[t] == t else want[t] for t in range(PP)])
    g.wait_ge(S.wr, 1)
    g.remote_dma_fused(
        [RemoteDMATransfer(dst_ids=[dst_id(mine[q]) for q in order[p]], dma_engine_mask=m3(p),
                           remote_sem=S["ya%d" % p], srcs=[piece(T.Y, p)], dsts=[piece(T.Y, p) for q in order[p]])],
        local_sem=S.sent)
    sent += len(_bits(m3(p)))

    if not own:
        v.wait_ge(S["ya%d" % hq], len(_bits(m3(hq))))
        acc(T.U[:], T.W[:], T.Y[:, rank * F:(rank + 1) * F], AluOpType.subtract)
        v.wait_ge(S.va, nva[0])
        v.tensor_tensor(T.MO[:], T.U[:], T.U[:], AluOpType.add).then_inc(S.mr, 1)

    arr = sorted(peers, key=lambda q: order[q].index(p))
    nsy = nsc = 0

    def put_mo():
        sy.wait_ge(S.mr, 1)
        sy.dma_start(T.mo[:], T.MO[:]).then_inc(S.sty, 16)

    sy.wait_ge(S.wr, 1)
    sy.dma_start(piece(T.y, p), piece(T.Y, p)).then_inc(S.sty, 16)
    nsy += 16
    if own:
        put_mo()
        nsy += 16
    for k, q in enumerate(arr):
        eng, sem = ((sc, S.stm), (sy, S.sty), (sc, S.stm))[k]
        eng.wait_ge(S["ya%d" % q], len(_bits(m3(q))))
        eng.dma_start(piece(T.y, q), piece(T.Y, q)).then_inc(sem, 16)
        if k == 1:
            nsy += 16
        else:
            nsc += 16
    if not own:
        put_mo()
        nsy += 16
    sy.wait_ge(S.sty, nsy)
    sc.wait_ge(S.stm, nsc)
    g.wait_ge(S.sent, sent)
